import numpy as np
import ml_dtypes

BF16 = ml_dtypes.bfloat16


def bf(x):
    return np.asarray(x, np.float32).astype(BF16)


def f32(x):
    return np.asarray(x, np.float32)


def f64(x):
    return np.asarray(x).astype(np.float64)


def striped(idx):
    return np.concatenate([l.reshape(-1, 16).T for l in idx])


def rows(idx, k):
    return np.tile(np.repeat(idx, 16, axis=0), (k // (16 * 8), 1))


def look(tab, idx):
    return np.take_along_axis(f64(tab), rows(idx, len(tab)), axis=1)


K, S, V, N, M = 512, 2048, 1536, 1536, 256


def setup_inputs():
    return {"tab": bf(np.random.standard_normal((K, S))), "w": bf(np.random.standard_normal((K, M)) / np.sqrt(K)), "b": f32(0.5 * np.random.standard_normal((M, 1))), "offs": striped(np.random.randint(0, S, (8, N)))}


def reference(tab, w, b, offs):
    idx = np.stack([g.T.reshape(-1) for g in np.split(offs, 8)])
    t = look(tab, idx)
    x = t
    y = f64(w).T @ x
    return y + f64(b)

@@ -1,0 +1,58 @@
+import concourse.mybir as mybir
+
+BF16, F32, U16 = mybir.dt.bfloat16, mybir.dt.float32, mybir.dt.uint16
+IDENTITY = mybir.ActivationFunctionType.Identity
+
+P = 128
+PIECE = 512
+LANES = 16
+
+FLOPS = 2 * 512 * 256 * 1536
+
+
+def tile_lookup_dec_copy_bias_kernel(tc, tab, w, b, offs, out):
+    nc = tc.nc
+    rows, codewords = tab.shape
+    features, vectors = out.shape
+    blocks = rows // P
+    halves = features // P
+    pieces = vectors // PIECE
+
+    with (
+        tc.tile_pool(name="held", bufs=1) as held,
+        tc.tile_pool(name="picked", bufs=4) as picked_pool,
+        tc.tile_pool(name="result", bufs=2) as result_pool,
+        tc.psum_pool(name="psum", bufs=1) as psum,
+    ):
+        lists = held.tile([P, vectors // LANES], U16, name="lists")
+        nc.sync.dma_start(lists[:], offs)
+        windows = [held.tile([P, codewords], BF16, name=f"window{k}") for k in range(blocks)]
+        nc.sync.dma_start(windows[0][:], tab[0:P, :])
+        weights = held.tile([P, blocks, features], BF16, name="weights")
+        nc.sync.dma_start(weights[:], w.rearrange("(k p) m -> p k m", p=P))
+        for k in range(1, blocks):
+            nc.sync.dma_start(windows[k][:], tab[k * P : (k + 1) * P, :])
+        bias = held.tile([P, halves], F32, name="bias")
+        nc.scalar.dma_start(bias[:], b.rearrange("(h p) o -> p (h o)", p=P))
+
+        sums = [[psum.tile([P, PIECE], F32, name=f"sum{h}_{j}") for j in range(pieces)] for h in range(halves)]
+
+        for k in range(blocks):
+            for j in range(pieces):
+                columns = slice(j * PIECE // LANES, (j + 1) * PIECE // LANES)
+                picked = picked_pool.tile([P, PIECE], BF16, name="picked")
+                nc.vector.tensor_copy(picked[:], windows[k][:].indirect(lists[:, columns]))
+                for h in range(halves):
+                    nc.tensor.matmul(
+                        sums[h][j][:],
+                        weights[:, k, h * P : (h + 1) * P],
+                        picked[:],
+                        start=(k == 0),
+                        stop=(k == blocks - 1),
+                    )
+
+        for j in range(pieces):
+            for h in range(halves):
+                result = result_pool.tile([P, PIECE], F32, name="result")
+                nc.scalar.activation(result[:], sums[h][j][:], IDENTITY, bias=bias[:, h : h + 1])
+                nc.sync.dma_start(out[h * P : (h + 1) * P, j * PIECE : (j + 1) * PIECE], result[:])

@@ -21,7 +21,7 @@ def tile_lookup_dec_copy_bias_kernel(tc, tab, w, b, offs, out):
     with (
         tc.tile_pool(name="held", bufs=1) as held,
         tc.tile_pool(name="picked", bufs=4) as picked_pool,
-        tc.tile_pool(name="result", bufs=2) as result_pool,
+        tc.tile_pool(name="result", bufs=1) as result_pool,
         tc.psum_pool(name="psum", bufs=1) as psum,
     ):
         lists = held.tile([P, vectors // LANES], U16, name="lists")
@@ -53,6 +53,9 @@ def tile_lookup_dec_copy_bias_kernel(tc, tab, w, b, offs, out):
 
         for j in range(pieces):
             for h in range(halves):
-                result = result_pool.tile([P, PIECE], F32, name="result")
-                nc.scalar.activation(result[:], sums[h][j][:], IDENTITY, bias=bias[:, h : h + 1])
+                result = result_pool.tile([P, PIECE], F32, name=f"result{h}_{j}")
+                if j == pieces - 1 and h == halves - 1:
+                    nc.vector.tensor_scalar_add(result[:], sums[h][j][:], bias[:, h : h + 1])
+                else:
+                    nc.scalar.activation(result[:], sums[h][j][:], IDENTITY, bias=bias[:, h : h + 1])
                 nc.sync.dma_start(out[h * P : (h + 1) * P, j * PIECE : (j + 1) * PIECE], result[:])

@@ -1,13 +1,18 @@
 import concourse.mybir as mybir
 
-BF16, F32, U16 = mybir.dt.bfloat16, mybir.dt.float32, mybir.dt.uint16
+BF16, F32, I32, U16 = mybir.dt.bfloat16, mybir.dt.float32, mybir.dt.int32, mybir.dt.uint16
 IDENTITY = mybir.ActivationFunctionType.Identity
 
 P = 128
 PIECE = 512
 LANES = 16
+PAIR = 2
 
 FLOPS = 2 * 512 * 256 * 1536
+
+
+def by_block(words):
+    return words[:].bitcast(BF16).rearrange("p (s t) -> p s t", t=PAIR)
 
 
 def tile_lookup_dec_copy_bias_kernel(tc, tab, w, b, offs, out):
@@ -15,6 +20,7 @@ def tile_lookup_dec_copy_bias_kernel(tc, tab, w, b, offs, out):
     rows, codewords = tab.shape
     features, vectors = out.shape
     blocks = rows // P
+    pairs = blocks // PAIR
     halves = features // P
     pieces = vectors // PIECE
 
@@ -24,32 +30,50 @@ def tile_lookup_dec_copy_bias_kernel(tc, tab, w, b, offs, out):
         tc.tile_pool(name="result", bufs=1) as result_pool,
         tc.psum_pool(name="psum", bufs=1) as psum,
     ):
+        loaded = [held.tile([P, codewords], BF16, name=f"loaded{k}") for k in range(blocks)]
+        for k in range(PAIR):
+            nc.sync.dma_start(loaded[k][:], tab[k * P : (k + 1) * P, :])
         lists = held.tile([P, vectors // LANES], U16, name="lists")
         nc.sync.dma_start(lists[:], offs)
-        windows = [held.tile([P, codewords], BF16, name=f"window{k}") for k in range(blocks)]
-        nc.sync.dma_start(windows[0][:], tab[0:P, :])
+        for k in range(PAIR, blocks):
+            nc.sync.dma_start(loaded[k][:], tab[k * P : (k + 1) * P, :])
         weights = held.tile([P, blocks, features], BF16, name="weights")
         nc.sync.dma_start(weights[:], w.rearrange("(k p) m -> p k m", p=P))
-        for k in range(1, blocks):
-            nc.sync.dma_start(windows[k][:], tab[k * P : (k + 1) * P, :])
         bias = held.tile([P, halves], F32, name="bias")
         nc.scalar.dma_start(bias[:], b.rearrange("(h p) o -> p (h o)", p=P))
 
+        windows = [held.tile([P, codewords], I32, name=f"window{q}") for q in range(pairs)]
+        third = codewords // 3 // 16 * 16
+        half = codewords // 2
+        for t in range(PAIR):
+            spread = by_block(windows[0])
+            nc.scalar.copy(spread[:, :third, t], loaded[t][:, :third])
+            nc.vector.tensor_copy(spread[:, third:, t], loaded[t][:, third:])
+        for q in range(1, pairs):
+            for t in range(PAIR):
+                spread = by_block(windows[q])
+                block = loaded[q * PAIR + t]
+                nc.scalar.copy(spread[:, :half, t], block[:, :half])
+                nc.gpsimd.tensor_copy(spread[:, half:, t], block[:, half:])
+
         sums = [[psum.tile([P, PIECE], F32, name=f"sum{h}_{j}") for j in range(pieces)] for h in range(halves)]
 
-        for k in range(blocks):
+        for q in range(pairs):
             for j in range(pieces):
                 columns = slice(j * PIECE // LANES, (j + 1) * PIECE // LANES)
-                picked = picked_pool.tile([P, PIECE], BF16, name="picked")
-                nc.vector.tensor_copy(picked[:], windows[k][:].indirect(lists[:, columns]))
+                picked = picked_pool.tile([P, PIECE], I32, name="picked")
+                nc.vector.tensor_copy(picked[:], windows[q][:].indirect(lists[:, columns]))
+                x = by_block(picked)
                 for h in range(halves):
-                    nc.tensor.matmul(
-                        sums[h][j][:],
-                        weights[:, k, h * P : (h + 1) * P],
-                        picked[:],
-                        start=(k == 0),
-                        stop=(k == blocks - 1),
-                    )
+                    for t in range(PAIR):
+                        k = q * PAIR + t
+                        nc.tensor.matmul(
+                            sums[h][j][:],
+                            weights[:, k, h * P : (h + 1) * P],
+                            x[:, :, t],
+                            start=(k == 0),
+                            stop=(k == blocks - 1),
+                        )
 
         for j in range(pieces):
             for h in range(halves):

@@ -6,6 +6,7 @@ IDENTITY = mybir.ActivationFunctionType.Identity
 P = 128
 PIECE = 512
 LANES = 16
+WARM_UPS = 16
 PAIR = 2
 
 FLOPS = 2 * 512 * 256 * 1536
@@ -55,6 +56,12 @@ def tile_lookup_dec_copy_bias_kernel(tc, tab, w, b, offs, out):
                 block = loaded[q * PAIR + t]
                 nc.scalar.copy(spread[:, :half, t], block[:, :half])
                 nc.gpsimd.tensor_copy(spread[:, half:, t], block[:, half:])
+
+        zeros = held.tile([P, PIECE], BF16, name="zeros")
+        nc.gpsimd.memset(zeros[:], 0.0)
+        warm = psum.tile([P, PIECE], F32, name="warm")
+        for i in range(WARM_UPS):
+            nc.tensor.matmul(warm[:], zeros[:, :P], zeros[:], start=True, stop=True)
 
         sums = [[psum.tile([P, PIECE], F32, name=f"sum{h}_{j}") for j in range(pieces)] for h in range(halves)]
 

@@ -7,6 +7,7 @@ P = 128
 PIECE = 512
 LANES = 16
 WARM_UPS = 16
+SLAB = 1024
 PAIR = 2
 
 FLOPS = 2 * 512 * 256 * 1536
@@ -32,8 +33,10 @@ def tile_lookup_dec_copy_bias_kernel(tc, tab, w, b, offs, out):
         tc.psum_pool(name="psum", bufs=1) as psum,
     ):
         loaded = [held.tile([P, codewords], BF16, name=f"loaded{k}") for k in range(blocks)]
-        for k in range(PAIR):
-            nc.sync.dma_start(loaded[k][:], tab[k * P : (k + 1) * P, :])
+        slabs = [slice(c, c + SLAB) for c in range(0, codewords, SLAB)]
+        for slab in slabs:
+            for t in range(PAIR):
+                nc.sync.dma_start(loaded[t][:, slab], tab[t * P : (t + 1) * P, slab])
         lists = held.tile([P, vectors // LANES], U16, name="lists")
         nc.sync.dma_start(lists[:], offs)
         for k in range(PAIR, blocks):
@@ -44,12 +47,14 @@ def tile_lookup_dec_copy_bias_kernel(tc, tab, w, b, offs, out):
         nc.scalar.dma_start(bias[:], b.rearrange("(h p) o -> p (h o)", p=P))
 
         windows = [held.tile([P, codewords], I32, name=f"window{q}") for q in range(pairs)]
-        third = codewords // 3 // 16 * 16
+        third = SLAB // 3 // 16 * 16
         half = codewords // 2
-        for t in range(PAIR):
-            spread = by_block(windows[0])
-            nc.scalar.copy(spread[:, :third, t], loaded[t][:, :third])
-            nc.vector.tensor_copy(spread[:, third:, t], loaded[t][:, third:])
+        for slab in slabs:
+            for t in range(PAIR):
+                spread = by_block(windows[0])[:, slab, t]
+                block = loaded[t][:, slab]
+                nc.scalar.copy(spread[:, :third], block[:, :third])
+                nc.vector.tensor_copy(spread[:, third:], block[:, third:])
         for q in range(1, pairs):
             for t in range(PAIR):
                 spread = by_block(windows[q])

import concourse.mybir as mybir

BF16, F32, I32, U16 = mybir.dt.bfloat16, mybir.dt.float32, mybir.dt.int32, mybir.dt.uint16
IDENTITY = mybir.ActivationFunctionType.Identity

P = 128
PIECE = 512
LANES = 16
WARM_UPS = 16
SLAB = 1024
PAIR = 2

FLOPS = 2 * 512 * 256 * 1536


def by_block(words):
    return words[:].bitcast(BF16).rearrange("p (s t) -> p s t", t=PAIR)


def tile_lookup_dec_copy_bias_kernel(tc, tab, w, b, offs, out):
    nc = tc.nc
    rows, codewords = tab.shape
    features, vectors = out.shape
    blocks = rows // P
    pairs = blocks // PAIR
    halves = features // P
    pieces = vectors // PIECE

    with (
        tc.tile_pool(name="held", bufs=1) as held,
        tc.tile_pool(name="picked", bufs=4) as picked_pool,
        tc.tile_pool(name="result", bufs=1) as result_pool,
        tc.psum_pool(name="psum", bufs=1) as psum,
    ):
        loaded = [held.tile([P, codewords], BF16, name=f"loaded{k}") for k in range(blocks)]
        slabs = [slice(c, c + SLAB) for c in range(0, codewords, SLAB)]
        for slab in slabs:
            for t in range(PAIR):
                nc.sync.dma_start(loaded[t][:, slab], tab[t * P : (t + 1) * P, slab])
        lists = held.tile([P, vectors // LANES], U16, name="lists")
        nc.sync.dma_start(lists[:], offs)
        for k in range(PAIR, blocks):
            nc.sync.dma_start(loaded[k][:], tab[k * P : (k + 1) * P, :])
        weights = held.tile([P, blocks, features], BF16, name="weights")
        nc.sync.dma_start(weights[:], w.rearrange("(k p) m -> p k m", p=P))
        bias = held.tile([P, halves], F32, name="bias")
        nc.scalar.dma_start(bias[:], b.rearrange("(h p) o -> p (h o)", p=P))

        windows = [held.tile([P, codewords], I32, name=f"window{q}") for q in range(pairs)]
        third = SLAB // 3 // 16 * 16
        half = codewords // 2
        for slab in slabs:
            for t in range(PAIR):
                spread = by_block(windows[0])[:, slab, t]
                block = loaded[t][:, slab]
                nc.scalar.copy(spread[:, :third], block[:, :third])
                nc.vector.tensor_copy(spread[:, third:], block[:, third:])
        for q in range(1, pairs):
            for t in range(PAIR):
                spread = by_block(windows[q])
                block = loaded[q * PAIR + t]
                nc.scalar.copy(spread[:, :half, t], block[:, :half])
                nc.gpsimd.tensor_copy(spread[:, half:, t], block[:, half:])

        zeros = held.tile([P, PIECE], BF16, name="zeros")
        nc.gpsimd.memset(zeros[:], 0.0)
        warm = psum.tile([P, PIECE], F32, name="warm")
        for i in range(WARM_UPS):
            nc.tensor.matmul(warm[:], zeros[:, :P], zeros[:], start=True, stop=True)

        sums = [[psum.tile([P, PIECE], F32, name=f"sum{h}_{j}") for j in range(pieces)] for h in range(halves)]

        for q in range(pairs):
            for j in range(pieces):
                columns = slice(j * PIECE // LANES, (j + 1) * PIECE // LANES)
                picked = picked_pool.tile([P, PIECE], I32, name="picked")
                nc.vector.tensor_copy(picked[:], windows[q][:].indirect(lists[:, columns]))
                x = by_block(picked)
                for h in range(halves):
                    for t in range(PAIR):
                        k = q * PAIR + t
                        nc.tensor.matmul(
                            sums[h][j][:],
                            weights[:, k, h * P : (h + 1) * P],
                            x[:, :, t],
                            start=(k == 0),
                            stop=(k == blocks - 1),
                        )

        for j in range(pieces):
            for h in range(halves):
                result = result_pool.tile([P, PIECE], F32, name=f"result{h}_{j}")
                if j == pieces - 1 and h == halves - 1:
                    nc.vector.tensor_scalar_add(result[:], sums[h][j][:], bias[:, h : h + 1])
                else:
                    nc.scalar.activation(result[:], sums[h][j][:], IDENTITY, bias=bias[:, h : h + 1])
                nc.sync.dma_start(out[h * P : (h + 1) * P, j * PIECE : (j + 1) * PIECE], result[:])
